import numpy as np, ml_dtypes
CORES = [113,118,241,246]
N = 4
import mx_ref
NC, G = 128, 2
C = np.float32(0.019)
BF = ml_dtypes.bfloat16
def cut(t, i, w=512):
    return t[:, w * i:w * i + w]
def tile(rs):
    return np.stack(rs, axis=2).reshape(128, -1).astype(BF)
def layer(w, X):
    out = []
    for i in range(G):
        for t in range(len(X)):
            p = mx_ref.matmul(mx_ref.quantize(cut(w, len(X) * i + t)), X[t])
            z = p if t == 0 else z + p
        out.append(z)
    return out
def act(Z):
    return [np.maximum(s * z, 0) * C for z in Z for s in (1, -1)]
def pick(b):
    s = np.zeros((128, 128, 4), np.float32)
    s[np.arange(128), np.arange(128), b] = 1.0
    return mx_ref.quantize(s.reshape(128, 512).astype(BF))
def setup_inputs(rng):
    def f(*shape):
        return mx_ref.flush((rng.standard_normal(shape, dtype=np.float32) * np.exp2(rng.integers(-2, 3, shape[:-1] + (1,)))).astype(BF))
    return {"a": f(N, 128, G * 512), "b": f(N, 128, N * 4 * NC), "gr": f(N, 128, N * 4 * NC)}
def setup_inputs_blocks(rng):
    d = setup_inputs(rng)
    for k in ("a", "b", "gr"): d[k] = mx_ref.spread(d[k], rng, 2)
    return d
def setup_inputs_wide(rng):
    d = setup_inputs(rng)
    for k in ("a", "b", "gr"): d[k] = mx_ref.flush((d[k].astype(np.float32) * np.exp2(rng.integers(-4, 5, (N, 1, 1))).astype(np.float32)).astype(BF))
    return d
def setup_inputs_zeros(rng):
    d = setup_inputs(rng); v = d["b"].reshape(N, 128, -1, 4).copy()
    v[np.broadcast_to((rng.random((N, 1, v.shape[2], 1)) < 0.33), v.shape)] = 0
    d["b"] = v.reshape(d["b"].shape)
    return d
def reference(a, b, gr):
    S = [pick(t) for t in range(4)]
    held = lambda q: [mx_ref.matmul(S[t], q) for t in range(4)]
    y = np.zeros((N, 128, NC, 4), np.float32); e = np.zeros((N, N, 128, NC, 4), np.float32)
    for c in range(N):
        for r in range(N):
            R = act(layer(a[r], [mx_ref.quantize(cut(b[r], c, 4 * NC))])); q = mx_ref.quantize(tile(R))
            D = held(q)
            e[r, c] = np.stack([R[t] - D[t] for t in range(4)], axis=2)
            p = np.stack(D if r == c else held(q), axis=2)
            q2 = mx_ref.quantize((cut(gr[r], c, 4 * NC).astype(np.float32) + e[r, c].reshape(128, -1)).astype(BF))
            p = p + np.stack(held(q2), axis=2)
            y[c] = p if r == 0 else y[c] + p
    return {"y": y.reshape(N, 128, 4 * NC)}

@@ -1,0 +1,291 @@
+import numpy as np
+from concourse.bass import DstId, RemoteDMATransfer
+from concourse.mybir import dt, AluOpType, ActivationFunctionType
+
+W = 128
+E4 = 4 * W
+BANK = 512
+SEL = E4 + 4
+CF = float(np.float32(0.019))
+F8 = "float8_e4m3fn_x4"
+
+SCRATCH = {
+    "at": ("sbuf", [128, 2 * E4], "bfloat16"),
+    "bt": ("sbuf", [128, 4 * E4], "bfloat16"),
+    "gt": ("sbuf", [128, 4 * E4], "bfloat16"),
+    "ones": ("sbuf", [128, SEL], "bfloat16"),
+    "sel": ("sbuf", [128, SEL], "bfloat16"),
+    "ht": ("sbuf", [128, 4 * E4], "bfloat16"),
+    "ut": ("sbuf", [128, 4 * E4], "bfloat16"),
+    "rf": ("sbuf", [128, 4 * E4], "float32"),
+    "df": ("sbuf", [128, E4], "float32"),
+    "yt": ("sbuf", [128, E4], "float32"),
+    "sc": ("sbuf", [128, 4 * W], F8), "ss": ("sbuf", [128, 4 * W], "uint8"),
+    "ac": ("sbuf", [128, 2 * W], F8), "as": ("sbuf", [128, 2 * W], "uint8"),
+    "bc": ("sbuf", [128, 4 * W], F8), "bs": ("sbuf", [128, 4 * W], "uint8"),
+    "qc": ("sbuf", [128, 4 * W], F8), "qs": ("sbuf", [128, 4 * W], "uint8"),
+    "uc": ("sbuf", [128, 4 * W], F8), "us": ("sbuf", [128, 4 * W], "uint8"),
+    "lqc": ("sbuf", [128, 4 * W], F8), "lqs": ("sbuf", [128, 4 * W], "uint8"),
+    "luc": ("sbuf", [128, 4 * W], F8), "lus": ("sbuf", [128, 4 * W], "uint8"),
+    "pz": ("psum", [128, 4 * BANK], "float32"),
+    "pd": ("psum", [128, 4 * BANK], "float32"),
+}
+LOADS = ["a0", "a1", "b0", "b1", "b2", "g0", "b3", "g1", "g2", "g3"]
+SEMAPHORES = (["pe", "dve", "act", "pool", "loc", "st"] + ["ld_" + n for n in LOADS]
+              + ["aq%d" % r for r in range(4)] + ["au%d" % r for r in range(4)])
+
+SENDS = [[("q", 0)], [("q", 1)], [("u", 0), ("q", 2)], [("u", 1)], [("u", 2)]]
+
+
+def bits(m):
+    return [e for e in range(m.bit_length()) if (m >> e) & 1]
+
+
+def join(es):
+    return sum(1 << e for e in es)
+
+
+def plan(topo, cores, src):
+    def here(d):
+        return topo.host(d) == topo.host(src) and topo.chip(d) == topo.chip(src)
+    far = sorted((d for d in cores if not here(d)), key=lambda d: topo.die(d) == topo.die(src))
+    near = [d for d in cores if here(d) and d != src]
+    order = far + near
+    out = bits(topo.mask(src, far[0]))
+    masks = {}
+    for group in SENDS:
+        going = [it for it in group if it[1] < len(far)]
+        for it in group:
+            if it in going:
+                share = len(out) // len(going)
+                i = going.index(it)
+                masks[it] = join(out[i * share:(i + 1) * share])
+            else:
+                masks[it] = join([e for e in bits(topo.mask(src, order[it[1]])) if e not in out])
+    return order, masks
+
+
+def engines(topo, cores, src, dst, kind):
+    order, masks = plan(topo, cores, src)
+    return len(bits(masks[(kind, order.index(dst))]))
+
+
+def rank_program(g, core, T, topo):
+    rank = T.rank_of(core)
+    if rank is None:
+        return
+    cores = list(T.cores)
+    order, masks = plan(topo, cores, core)
+    ranks = [T.rank_of(d) for d in order] + [rank]
+
+    queues = {"sync": g.sync, "act": g.scalar, "dve": g.vector, "pe": g.tensor, "pool": g}
+    progs = {q: [] for q in queues}
+    tok, count = {}, {}
+
+    def op(q, label, needs, call, sem=None, n=1, sig=True):
+        if sig:
+            s = sem or q
+            count[s] = count.get(s, 0) + n
+            tok[label] = (s, count[s])
+        progs[q].append((label, needs, call, (s, n) if sig else None))
+
+    def tl(name, k):
+        return T[name][:, E4 * k:E4 * (k + 1)]
+
+    def tb(name, k, b):
+        return T[name][:, E4 * k + b:E4 * (k + 1):4]
+
+    def wd(name, k):
+        return T[name][:, W * k:W * (k + 1)]
+
+    def bk(name, i):
+        return T[name][:, BANK * i:BANK * i + W]
+
+    def load(q, n):
+        kind, k = n[0], int(n[1])
+        src = T.a[:, E4 * k:E4 * (k + 1)] if kind == "a" else (T.b if kind == "b" else T.gr)[:, E4 * ranks[k]:E4 * (ranks[k] + 1)]
+        dst = tl(kind + "t", k)
+        op(q, "ld_" + n, [], lambda: queues[q].dma_start(dst, src), sem="ld_" + n, n=16)
+
+    for i, n in enumerate(LOADS):
+        load("sync" if i % 2 == 0 or i > 6 else "act", n)
+
+    op("dve", "ones", [], lambda: g.vector.memset(T.ones[:], 1.0))
+    op("pool", "sel", ["ones"], lambda: g.affine_select(T.sel[:], T.ones[:], [[-1, SEL]], AluOpType.is_equal, 0.0, 3, 4))
+
+    def quant(label, needs, c, s, k, src):
+        op("dve", label, needs, lambda: g.vector.quantize_mx(wd(c, k), wd(s, k), src))
+
+    def v_relu(k, b):
+        z = 2 * (k % 2) + b // 2
+        op("dve", "h%d%d" % (k, b), ["z%d%d" % (k, b // 2)], lambda: g.vector.tensor_scalar(
+            tb("ht", k, b), bk("pz", z), CF if b % 2 == 0 else -CF, 0.0, AluOpType.mult, AluOpType.max))
+
+    def q_in(n):
+        quant("q" + n, ["ld_" + n], n[0] + "c", n[0] + "s", int(n[1]), tl(n[0] + "t", int(n[1])))
+
+    def q_first(k):
+        quant("qq%d" % k, ["h%d%d" % (k, b) for b in range(4)], "qc", "qs", k, tl("ht", k))
+
+    def q_second(k):
+        quant("qu%d" % k, ["u%d" % k], "uc", "us", k, tl("ut", k))
+
+    def err(k, b):
+        op("dve", "e%d%d" % (k, b), ["d%d%d" % (k, b), "r%d%d" % (k, b)] + (["dcopy%d" % b] if k == 3 else []),
+           lambda: g.vector.tensor_tensor(tb("rf", k, b), tb("rf", k, b), bk("pd", b), AluOpType.subtract))
+
+    def add(k):
+        op("dve", "u%d" % k, ["e%d%d" % (k, b) for b in range(4)] + ["ld_g%d" % k],
+           lambda: g.vector.tensor_tensor(tl("ut", k), tl("gt", k), tl("rf", k), AluOpType.add))
+
+    for b in range(4):
+        quant("qS%d" % b, ["sel"], "sc", "ss", b, T.sel[:, 3 - b:3 - b + E4])
+    q_in("a0")
+    q_in("a1")
+    q_in("b0")
+    v_relu(0, 2)
+    v_relu(0, 3)
+    q_first(0)
+    q_in("b1")
+    for b in range(4):
+        err(0, b)
+    q_in("b2")
+    q_first(1)
+    add(0)
+    q_first(2)
+    q_second(0)
+    for b in range(4):
+        err(1, b)
+    q_in("b3")
+    add(1)
+    err(2, 0)
+    q_second(1)
+    for b in range(1, 4):
+        err(2, b)
+    q_first(3)
+    add(2)
+    q_second(2)
+    for b in range(4):
+        err(3, b)
+    add(3)
+    q_second(3)
+
+    def s_relu(pre, name, k, b):
+        z = 2 * (k % 2) + b // 2
+        needs = ["z%d%d" % (k, b // 2)]
+        if pre == "r" and k == 0 and b >= 2:
+            needs += ["h02", "h03"]
+        op("act", "%s%d%d" % (pre, k, b), needs, lambda: g.scalar.activation(
+            tb(name, k, b), bk("pz", z), ActivationFunctionType.Relu, scale=CF if b % 2 == 0 else -CF))
+
+    for pre, name, k, bs in (("h", "ht", 0, (0, 1)), ("r", "rf", 0, (0, 1, 2, 3)), ("h", "ht", 1, (0, 1, 2, 3)),
+                             ("h", "ht", 2, (0, 1, 2, 3)), ("r", "rf", 1, (0, 1, 2, 3)), ("r", "rf", 2, (0, 1, 2, 3)),
+                             ("h", "ht", 3, (0, 1, 2, 3)), ("r", "rf", 3, (0, 1, 2, 3))):
+        for b in bs:
+            s_relu(pre, name, k, b)
+    for b in range(4):
+        op("act", "dcopy%d" % b, ["d3%d" % b], lambda b=b: g.scalar.activation(
+            tb("df", 0, b), bk("pd", b), ActivationFunctionType.Copy))
+
+    def mm(label, needs, out, lc, ls, i, rc, rs, j, start, stop):
+        op("pe", label, needs, lambda: g.tensor.matmul_mx(out, wd(lc, i), wd(ls, i), wd(rc, j), wd(rs, j), start, stop))
+
+    def prod(k):
+        for i in range(2):
+            needs = ["qa%d" % i, "qb%d" % k]
+            if k >= 2:
+                needs += [p + "%d%d" % (k - 2, 2 * i + s) for p in "hr" for s in (0, 1)]
+            mm("z%d%d" % (k, i), needs, bk("pz", 2 * (k % 2) + i), "ac", "as", i, "bc", "bs", k, True, True)
+
+    def held(k):
+        for b in range(4):
+            needs = ["qS%d" % b, "qq%d" % k] + (["e%d%d" % (k - 1, b)] if k else [])
+            mm("d%d%d" % (k, b), needs, bk("pd", b), "sc", "ss", b, "qc", "qs", k, True, True)
+
+    prod(0)
+    prod(1)
+    held(0)
+    prod(2)
+    held(1)
+    prod(3)
+    held(2)
+    held(3)
+    for r in ranks[:3]:
+        for kind in "qu":
+            tok["a%s%d" % (kind, r)] = ("a%s%d" % (kind, r), 2 * engines(topo, cores, cores[r], core, kind))
+    slices = [("q", r) for r in ranks[:3]] + [("u", ranks[0]), ("u", ranks[1]), ("u", rank), ("u", ranks[2])]
+    free = ["%s%d%d" % (p, k, b) for p in "hr" for k in (2, 3) for b in range(4)]
+    for i, (kind, r) in enumerate(slices):
+        buf, j, need = ("u", 3, "qu3") if r == rank else ("l" + kind, r, "a%s%d" % (kind, r))
+        for b in range(4):
+            mm("s%d%d" % (i, b), [need] + (free if i == 0 else []), bk("pz", b), "sc", "ss", b,
+               buf + "c", buf + "s", j, i == 0, i == len(slices) - 1)
+
+    def send(group):
+        needs = ["q%s%d" % it for it in group]
+        for plane in "cs":
+            def view(buf, k, plane=plane):
+                v = wd(buf, k)
+                return v.bitcast(dt.uint8) if plane == "c" else v
+
+            def call(view=view, plane=plane):
+                tr = []
+                for kind, k in group:
+                    rid, pid = topo.addr(order[k], core)
+                    tr.append(RemoteDMATransfer(
+                        dst_ids=[DstId(rid=rid, pnc=pid)], dma_engine_mask=masks[(kind, k)], remote_sem=T.sem["a%s%d" % (kind, rank)],
+                        src=view(kind + plane, k), dst=view("l" + kind + plane, rank)))
+                return g.remote_dma_fused(tr, local_sem=T.sem.loc)
+            op("pool", "", needs, call, sig=False)
+            count["loc"] = count.get("loc", 0) + sum(len(bits(masks[it])) for it in group)
+
+    for group in SENDS:
+        send(group)
+
+    for b in range(4):
+        op("dve", "y%d" % b, ["s%d%d" % (len(slices) - 1, b), "dcopy%d" % b], lambda b=b: g.vector.tensor_tensor(
+            tb("yt", 0, b), tb("df", 0, b), bk("pz", b), AluOpType.add))
+    op("sync", "st", ["y%d" % b for b in range(4)], lambda: g.sync.dma_start(T.y[:], T.yt[:]), sem="st", n=16)
+
+    tok["loc"] = ("loc", count["loc"])
+    op("pool", "", ["loc"], None, sig=False)
+    op("sync", "", ["st"], None, sig=False)
+
+    emit(T, queues, progs, tok)
+
+
+def emit(T, queues, progs, tok):
+    known = {q: {} for q in queues}
+    clock = {sv: {sv[0]: sv[1]} for sv in tok.values() if sv[0][:2] in ("aq", "au", "lo")}
+    at = {q: 0 for q in queues}
+    left = sum(len(p) for p in progs.values())
+    while left:
+        moved = False
+        for q in queues:
+            while at[q] < len(progs[q]):
+                label, needs, call, sig = progs[q][at[q]]
+                want = {}
+                for n in needs:
+                    s, v = tok[n]
+                    want[s] = max(v, want.get(s, 0))
+                if any(sv not in clock for sv in want.items()):
+                    break
+                have = known[q]
+                for s, v in sorted(want.items(), key=lambda x: -len(clock[x])):
+                    if have.get(s, 0) < v:
+                        queues[q].wait_ge(T.sem[s], v)
+                        for s2, v2 in clock[(s, v)].items():
+                            have[s2] = max(v2, have.get(s2, 0))
+                if call is not None:
+                    ins = call()
+                    if sig is not None:
+                        ins.then_inc(T.sem[sig[0]], sig[1])
+                        c = dict(have)
+                        c[sig[0]] = max(c.get(sig[0], 0), tok[label][1])
+                        clock[tok[label]] = c
+                at[q] += 1
+                left -= 1
+                moved = True
+        if not moved:
+            raise RuntimeError("the queues wait for one another: " + ", ".join(
+                progs[q][at[q]][0] for q in queues if at[q] < len(progs[q])))

@@ -30,10 +30,14 @@ SCRATCH = {
     "pz": ("psum", [128, 4 * BANK], "float32"),
     "pd": ("psum", [128, 4 * BANK], "float32"),
 }
-LOADS = ["a0", "a1", "b0", "b1", "b2", "g0", "b3", "g1", "g2", "g3"]
-SEMAPHORES = (["pe", "dve", "act", "pool", "loc", "st"] + ["ld_" + n for n in LOADS]
+LOADS = [("sync", "a"), ("act", "b0"), ("sync", "b1"), ("act", "b2"), ("sync", "g0"), ("act", "b3"), ("sync", "g1"), ("sync", "g2")]
+SEMAPHORES = (["pe", "dve", "act", "pool", "loc", "st"] + ["ld_" + n for _, n in LOADS]
               + ["aq%d" % r for r in range(4)] + ["au%d" % r for r in range(4)])
 
+VECTOR = "I0 H023 F0 I1 I2 E0 I3 A0 F1 U0 F2 E1 A1 U1 E2 F3 A2 U2 E3 A3 U3"
+TENSOR = "z0 d0 z1 z2 d1 z3 d2 s0 d3 s1 s2 s3 s4 s5 s6"
+SLICES = [("q", 0), ("q", 2), ("q", 1), ("u", 0), ("u", 3), ("u", 1), ("u", 2)]
+SCALAR = "h001 r0 h1 h2 r1 r2 h3 r3"
 SENDS = [[("q", 0)], [("q", 1)], [("u", 0), ("q", 2)], [("u", 1)], [("u", 2)]]
 
 
@@ -54,14 +58,14 @@ def plan(topo, cores, src):
     out = bits(topo.mask(src, far[0]))
     masks = {}
     for group in SENDS:
-        going = [it for it in group if it[1] < len(far)]
+        going = [it for it in group if order[it[1]] in far]
         for it in group:
             if it in going:
                 share = len(out) // len(going)
                 i = going.index(it)
                 masks[it] = join(out[i * share:(i + 1) * share])
             else:
-                masks[it] = join([e for e in bits(topo.mask(src, order[it[1]])) if e not in out])
+                masks[it] = join([e for e in bits(topo.mask(src, order[it[1]])) if not going or e not in out])
     return order, masks
 
 
@@ -101,14 +105,26 @@ def rank_program(g, core, T, topo):
     def bk(name, i):
         return T[name][:, BANK * i:BANK * i + W]
 
+    def steps(text):
+        return [(w[0], int(w[1]), [int(x) for x in w[2:]] or [0, 1, 2, 3]) for w in text.split()]
+
+    low = min(ranks[2], ranks[3])
+    place = [0, 1] + [2 + r - low for r in ranks[2:]]
+
     def load(q, n):
-        kind, k = n[0], int(n[1])
-        src = T.a[:, E4 * k:E4 * (k + 1)] if kind == "a" else (T.b if kind == "b" else T.gr)[:, E4 * ranks[k]:E4 * (ranks[k] + 1)]
-        dst = tl(kind + "t", k)
+        if n == "a":
+            dst, src = T["at"][:], T.a[:]
+        elif n == "g2":
+            dst, src = T["gt"][:, 2 * E4:4 * E4], T.gr[:, E4 * low:E4 * (low + 2)]
+        else:
+            k = int(n[1])
+            dst = tl(n[0] + "t", k)
+            src = (T.b if n[0] == "b" else T.gr)[:, E4 * ranks[k]:E4 * (ranks[k] + 1)]
         op(q, "ld_" + n, [], lambda: queues[q].dma_start(dst, src), sem="ld_" + n, n=16)
 
-    for i, n in enumerate(LOADS):
-        load("sync" if i % 2 == 0 or i > 6 else "act", n)
+    for q, n in LOADS:
+        load(q, n)
+    tok["ld_g3"] = tok["ld_g2"]
 
     op("dve", "ones", [], lambda: g.vector.memset(T.ones[:], 1.0))
     op("pool", "sel", ["ones"], lambda: g.affine_select(T.sel[:], T.ones[:], [[-1, SEL]], AluOpType.is_equal, 0.0, 3, 4))
@@ -121,105 +137,67 @@ def rank_program(g, core, T, topo):
         op("dve", "h%d%d" % (k, b), ["z%d%d" % (k, b // 2)], lambda: g.vector.tensor_scalar(
             tb("ht", k, b), bk("pz", z), CF if b % 2 == 0 else -CF, 0.0, AluOpType.mult, AluOpType.max))
 
-    def q_in(n):
-        quant("q" + n, ["ld_" + n], n[0] + "c", n[0] + "s", int(n[1]), tl(n[0] + "t", int(n[1])))
-
-    def q_first(k):
-        quant("qq%d" % k, ["h%d%d" % (k, b) for b in range(4)], "qc", "qs", k, tl("ht", k))
-
-    def q_second(k):
-        quant("qu%d" % k, ["u%d" % k], "uc", "us", k, tl("ut", k))
-
     def err(k, b):
-        op("dve", "e%d%d" % (k, b), ["d%d%d" % (k, b), "r%d%d" % (k, b)] + (["dcopy%d" % b] if k == 3 else []),
+        op("dve", "e%d%d" % (k, b), ["d%d%d" % (k, b), "r%d%d" % (k, b)],
            lambda: g.vector.tensor_tensor(tb("rf", k, b), tb("rf", k, b), bk("pd", b), AluOpType.subtract))
 
     def add(k):
         op("dve", "u%d" % k, ["e%d%d" % (k, b) for b in range(4)] + ["ld_g%d" % k],
-           lambda: g.vector.tensor_tensor(tl("ut", k), tl("gt", k), tl("rf", k), AluOpType.add))
+           lambda: g.vector.tensor_tensor(tl("ut", k), tl("gt", place[k]), tl("rf", k), AluOpType.add))
 
     for b in range(4):
         quant("qS%d" % b, ["sel"], "sc", "ss", b, T.sel[:, 3 - b:3 - b + E4])
-    q_in("a0")
-    q_in("a1")
-    q_in("b0")
-    v_relu(0, 2)
-    v_relu(0, 3)
-    q_first(0)
-    q_in("b1")
-    for b in range(4):
-        err(0, b)
-    q_in("b2")
-    q_first(1)
-    add(0)
-    q_first(2)
-    q_second(0)
-    for b in range(4):
-        err(1, b)
-    q_in("b3")
-    add(1)
-    err(2, 0)
-    q_second(1)
-    for b in range(1, 4):
-        err(2, b)
-    q_first(3)
-    add(2)
-    q_second(2)
-    for b in range(4):
-        err(3, b)
-    add(3)
-    q_second(3)
+    for i in range(2):
+        quant("qa%d" % i, ["ld_a"], "ac", "as", i, tl("at", i))
+    for what, k, bs in steps(VECTOR):
+        if what == "I":
+            quant("qb%d" % k, ["ld_b%d" % k], "bc", "bs", k, tl("bt", k))
+        elif what == "F":
+            quant("qq%d" % k, ["h%d%d" % (k, b) for b in range(4)], "qc", "qs", k, tl("ht", k))
+        elif what == "U":
+            quant("qu%d" % k, ["u%d" % k], "uc", "us", k, tl("ut", k))
+        elif what == "A":
+            add(k)
+        else:
+            for b in bs:
+                (v_relu if what == "H" else err)(k, b)
 
-    def s_relu(pre, name, k, b):
-        z = 2 * (k % 2) + b // 2
-        needs = ["z%d%d" % (k, b // 2)]
-        if pre == "r" and k == 0 and b >= 2:
-            needs += ["h02", "h03"]
-        op("act", "%s%d%d" % (pre, k, b), needs, lambda: g.scalar.activation(
-            tb(name, k, b), bk("pz", z), ActivationFunctionType.Relu, scale=CF if b % 2 == 0 else -CF))
-
-    for pre, name, k, bs in (("h", "ht", 0, (0, 1)), ("r", "rf", 0, (0, 1, 2, 3)), ("h", "ht", 1, (0, 1, 2, 3)),
-                             ("h", "ht", 2, (0, 1, 2, 3)), ("r", "rf", 1, (0, 1, 2, 3)), ("r", "rf", 2, (0, 1, 2, 3)),
-                             ("h", "ht", 3, (0, 1, 2, 3)), ("r", "rf", 3, (0, 1, 2, 3))):
+    for what, k, bs in steps(SCALAR):
         for b in bs:
-            s_relu(pre, name, k, b)
+            needs = ["z%d%d" % (k, b // 2)]
+            if what == "r" and k == 0 and b >= 2:
+                needs += ["h02", "h03"]
+            op("act", "%s%d%d" % (what, k, b), needs, lambda k=k, b=b, name={"h": "ht", "r": "rf"}[what]: g.scalar.activation(
+                tb(name, k, b), bk("pz", 2 * (k % 2) + b // 2), ActivationFunctionType.Relu, scale=CF if b % 2 == 0 else -CF))
     for b in range(4):
-        op("act", "dcopy%d" % b, ["d3%d" % b], lambda b=b: g.scalar.activation(
+        op("act", "dcopy%d" % b, ["d3%d" % b, "e3%d" % b], lambda b=b: g.scalar.activation(
             tb("df", 0, b), bk("pd", b), ActivationFunctionType.Copy))
 
     def mm(label, needs, out, lc, ls, i, rc, rs, j, start, stop):
         op("pe", label, needs, lambda: g.tensor.matmul_mx(out, wd(lc, i), wd(ls, i), wd(rc, j), wd(rs, j), start, stop))
 
-    def prod(k):
-        for i in range(2):
-            needs = ["qa%d" % i, "qb%d" % k]
-            if k >= 2:
-                needs += [p + "%d%d" % (k - 2, 2 * i + s) for p in "hr" for s in (0, 1)]
-            mm("z%d%d" % (k, i), needs, bk("pz", 2 * (k % 2) + i), "ac", "as", i, "bc", "bs", k, True, True)
-
-    def held(k):
-        for b in range(4):
-            needs = ["qS%d" % b, "qq%d" % k] + (["e%d%d" % (k - 1, b)] if k else [])
-            mm("d%d%d" % (k, b), needs, bk("pd", b), "sc", "ss", b, "qc", "qs", k, True, True)
-
-    prod(0)
-    prod(1)
-    held(0)
-    prod(2)
-    held(1)
-    prod(3)
-    held(2)
-    held(3)
     for r in ranks[:3]:
         for kind in "qu":
             tok["a%s%d" % (kind, r)] = ("a%s%d" % (kind, r), 2 * engines(topo, cores, cores[r], core, kind))
-    slices = [("q", r) for r in ranks[:3]] + [("u", ranks[0]), ("u", ranks[1]), ("u", rank), ("u", ranks[2])]
+    last = len(SLICES) - 1
     free = ["%s%d%d" % (p, k, b) for p in "hr" for k in (2, 3) for b in range(4)]
-    for i, (kind, r) in enumerate(slices):
-        buf, j, need = ("u", 3, "qu3") if r == rank else ("l" + kind, r, "a%s%d" % (kind, r))
-        for b in range(4):
-            mm("s%d%d" % (i, b), [need] + (free if i == 0 else []), bk("pz", b), "sc", "ss", b,
-               buf + "c", buf + "s", j, i == 0, i == len(slices) - 1)
+    for what, k, bs in steps(TENSOR):
+        if what == "z":
+            for i in range(2):
+                needs = ["qa%d" % i, "qb%d" % k]
+                if k >= 2:
+                    needs += [p + "%d%d" % (k - 2, 2 * i + s) for p in "hr" for s in (0, 1)]
+                mm("z%d%d" % (k, i), needs, bk("pz", 2 * (k % 2) + i), "ac", "as", i, "bc", "bs", k, True, True)
+        elif what == "d":
+            for b in bs:
+                needs = ["qS%d" % b, "qq%d" % k] + (["e%d%d" % (k - 1, b)] if k else [])
+                mm("d%d%d" % (k, b), needs, bk("pd", b), "sc", "ss", b, "qc", "qs", k, True, True)
+        else:
+            kind, r = SLICES[k][0], ranks[SLICES[k][1]]
+            buf, j, need = ("u", 3, "qu3") if r == rank else ("l" + kind, r, "a%s%d" % (kind, r))
+            for b in bs:
+                mm("s%d%d" % (k, b), [need] + (free if k == 0 else []), bk("pz", b), "sc", "ss", b,
+                   buf + "c", buf + "s", j, k == 0, k == last)
 
     def send(group):
         needs = ["q%s%d" % it for it in group]
@@ -243,7 +221,7 @@ def rank_program(g, core, T, topo):
         send(group)
 
     for b in range(4):
-        op("dve", "y%d" % b, ["s%d%d" % (len(slices) - 1, b), "dcopy%d" % b], lambda b=b: g.vector.tensor_tensor(
+        op("dve", "y%d" % b, ["s%d%d" % (last, b), "dcopy%d" % b], lambda b=b: g.vector.tensor_tensor(
             tb("yt", 0, b), tb("df", 0, b), bk("pz", b), AluOpType.add))
     op("sync", "st", ["y%d" % b for b in range(4)], lambda: g.sync.dma_start(T.y[:], T.yt[:]), sem="st", n=16)
 

import numpy as np
from concourse.bass import DstId, RemoteDMATransfer
from concourse.mybir import dt, AluOpType, ActivationFunctionType

W = 128
E4 = 4 * W
BANK = 512
SEL = E4 + 4
CF = float(np.float32(0.019))
F8 = "float8_e4m3fn_x4"

SCRATCH = {
    "at": ("sbuf", [128, 2 * E4], "bfloat16"),
    "bt": ("sbuf", [128, 4 * E4], "bfloat16"),
    "gt": ("sbuf", [128, 4 * E4], "bfloat16"),
    "ones": ("sbuf", [128, SEL], "bfloat16"),
    "sel": ("sbuf", [128, SEL], "bfloat16"),
    "ht": ("sbuf", [128, 4 * E4], "bfloat16"),
    "ut": ("sbuf", [128, 4 * E4], "bfloat16"),
    "rf": ("sbuf", [128, 4 * E4], "float32"),
    "df": ("sbuf", [128, E4], "float32"),
    "yt": ("sbuf", [128, E4], "float32"),
    "sc": ("sbuf", [128, 4 * W], F8), "ss": ("sbuf", [128, 4 * W], "uint8"),
    "ac": ("sbuf", [128, 2 * W], F8), "as": ("sbuf", [128, 2 * W], "uint8"),
    "bc": ("sbuf", [128, 4 * W], F8), "bs": ("sbuf", [128, 4 * W], "uint8"),
    "qc": ("sbuf", [128, 4 * W], F8), "qs": ("sbuf", [128, 4 * W], "uint8"),
    "uc": ("sbuf", [128, 4 * W], F8), "us": ("sbuf", [128, 4 * W], "uint8"),
    "lqc": ("sbuf", [128, 4 * W], F8), "lqs": ("sbuf", [128, 4 * W], "uint8"),
    "luc": ("sbuf", [128, 4 * W], F8), "lus": ("sbuf", [128, 4 * W], "uint8"),
    "pz": ("psum", [128, 4 * BANK], "float32"),
    "pd": ("psum", [128, 4 * BANK], "float32"),
}
LOADS = [("sync", "a"), ("act", "b0"), ("sync", "b1"), ("act", "b2"), ("sync", "g0"), ("act", "b3"), ("sync", "g1"), ("sync", "g2")]
SEMAPHORES = (["pe", "dve", "act", "pool", "loc", "st"] + ["ld_" + n for _, n in LOADS]
              + ["aq%d" % r for r in range(4)] + ["au%d" % r for r in range(4)])

VECTOR = "I0 H023 F0 I1 I2 E0 I3 A0 F1 U0 F2 E1 A1 U1 E2 F3 A2 U2 E3 A3 U3"
TENSOR = "z0 d0 z1 z2 d1 z3 d2 s0 d3 s1 s2 s3 s4 s5 s6"
SLICES = [("q", 0), ("q", 2), ("q", 1), ("u", 0), ("u", 3), ("u", 1), ("u", 2)]
SCALAR = "h001 r0 h1 h2 r1 r2 h3 r3"
SENDS = [[("q", 0)], [("q", 1)], [("u", 0), ("q", 2)], [("u", 1)], [("u", 2)]]


def bits(m):
    return [e for e in range(m.bit_length()) if (m >> e) & 1]


def join(es):
    return sum(1 << e for e in es)


def plan(topo, cores, src):
    def here(d):
        return topo.host(d) == topo.host(src) and topo.chip(d) == topo.chip(src)
    far = sorted((d for d in cores if not here(d)), key=lambda d: topo.die(d) == topo.die(src))
    near = [d for d in cores if here(d) and d != src]
    order = far + near
    out = bits(topo.mask(src, far[0]))
    masks = {}
    for group in SENDS:
        going = [it for it in group if order[it[1]] in far]
        for it in group:
            if it in going:
                share = len(out) // len(going)
                i = going.index(it)
                masks[it] = join(out[i * share:(i + 1) * share])
            else:
                masks[it] = join([e for e in bits(topo.mask(src, order[it[1]])) if not going or e not in out])
    return order, masks


def engines(topo, cores, src, dst, kind):
    order, masks = plan(topo, cores, src)
    return len(bits(masks[(kind, order.index(dst))]))


def rank_program(g, core, T, topo):
    rank = T.rank_of(core)
    if rank is None:
        return
    cores = list(T.cores)
    order, masks = plan(topo, cores, core)
    ranks = [T.rank_of(d) for d in order] + [rank]

    queues = {"sync": g.sync, "act": g.scalar, "dve": g.vector, "pe": g.tensor, "pool": g}
    progs = {q: [] for q in queues}
    tok, count = {}, {}

    def op(q, label, needs, call, sem=None, n=1, sig=True):
        if sig:
            s = sem or q
            count[s] = count.get(s, 0) + n
            tok[label] = (s, count[s])
        progs[q].append((label, needs, call, (s, n) if sig else None))

    def tl(name, k):
        return T[name][:, E4 * k:E4 * (k + 1)]

    def tb(name, k, b):
        return T[name][:, E4 * k + b:E4 * (k + 1):4]

    def wd(name, k):
        return T[name][:, W * k:W * (k + 1)]

    def bk(name, i):
        return T[name][:, BANK * i:BANK * i + W]

    def steps(text):
        return [(w[0], int(w[1]), [int(x) for x in w[2:]] or [0, 1, 2, 3]) for w in text.split()]

    low = min(ranks[2], ranks[3])
    place = [0, 1] + [2 + r - low for r in ranks[2:]]

    def load(q, n):
        if n == "a":
            dst, src = T["at"][:], T.a[:]
        elif n == "g2":
            dst, src = T["gt"][:, 2 * E4:4 * E4], T.gr[:, E4 * low:E4 * (low + 2)]
        else:
            k = int(n[1])
            dst = tl(n[0] + "t", k)
            src = (T.b if n[0] == "b" else T.gr)[:, E4 * ranks[k]:E4 * (ranks[k] + 1)]
        op(q, "ld_" + n, [], lambda: queues[q].dma_start(dst, src), sem="ld_" + n, n=16)

    for q, n in LOADS:
        load(q, n)
    tok["ld_g3"] = tok["ld_g2"]

    op("dve", "ones", [], lambda: g.vector.memset(T.ones[:], 1.0))
    op("pool", "sel", ["ones"], lambda: g.affine_select(T.sel[:], T.ones[:], [[-1, SEL]], AluOpType.is_equal, 0.0, 3, 4))

    def quant(label, needs, c, s, k, src):
        op("dve", label, needs, lambda: g.vector.quantize_mx(wd(c, k), wd(s, k), src))

    def v_relu(k, b):
        z = 2 * (k % 2) + b // 2
        op("dve", "h%d%d" % (k, b), ["z%d%d" % (k, b // 2)], lambda: g.vector.tensor_scalar(
            tb("ht", k, b), bk("pz", z), CF if b % 2 == 0 else -CF, 0.0, AluOpType.mult, AluOpType.max))

    def err(k, b):
        op("dve", "e%d%d" % (k, b), ["d%d%d" % (k, b), "r%d%d" % (k, b)],
           lambda: g.vector.tensor_tensor(tb("rf", k, b), tb("rf", k, b), bk("pd", b), AluOpType.subtract))

    def add(k):
        op("dve", "u%d" % k, ["e%d%d" % (k, b) for b in range(4)] + ["ld_g%d" % k],
           lambda: g.vector.tensor_tensor(tl("ut", k), tl("gt", place[k]), tl("rf", k), AluOpType.add))

    for b in range(4):
        quant("qS%d" % b, ["sel"], "sc", "ss", b, T.sel[:, 3 - b:3 - b + E4])
    for i in range(2):
        quant("qa%d" % i, ["ld_a"], "ac", "as", i, tl("at", i))
    for what, k, bs in steps(VECTOR):
        if what == "I":
            quant("qb%d" % k, ["ld_b%d" % k], "bc", "bs", k, tl("bt", k))
        elif what == "F":
            quant("qq%d" % k, ["h%d%d" % (k, b) for b in range(4)], "qc", "qs", k, tl("ht", k))
        elif what == "U":
            quant("qu%d" % k, ["u%d" % k], "uc", "us", k, tl("ut", k))
        elif what == "A":
            add(k)
        else:
            for b in bs:
                (v_relu if what == "H" else err)(k, b)

    for what, k, bs in steps(SCALAR):
        for b in bs:
            needs = ["z%d%d" % (k, b // 2)]
            if what == "r" and k == 0 and b >= 2:
                needs += ["h02", "h03"]
            op("act", "%s%d%d" % (what, k, b), needs, lambda k=k, b=b, name={"h": "ht", "r": "rf"}[what]: g.scalar.activation(
                tb(name, k, b), bk("pz", 2 * (k % 2) + b // 2), ActivationFunctionType.Relu, scale=CF if b % 2 == 0 else -CF))
    for b in range(4):
        op("act", "dcopy%d" % b, ["d3%d" % b, "e3%d" % b], lambda b=b: g.scalar.activation(
            tb("df", 0, b), bk("pd", b), ActivationFunctionType.Copy))

    def mm(label, needs, out, lc, ls, i, rc, rs, j, start, stop):
        op("pe", label, needs, lambda: g.tensor.matmul_mx(out, wd(lc, i), wd(ls, i), wd(rc, j), wd(rs, j), start, stop))

    for r in ranks[:3]:
        for kind in "qu":
            tok["a%s%d" % (kind, r)] = ("a%s%d" % (kind, r), 2 * engines(topo, cores, cores[r], core, kind))
    last = len(SLICES) - 1
    free = ["%s%d%d" % (p, k, b) for p in "hr" for k in (2, 3) for b in range(4)]
    for what, k, bs in steps(TENSOR):
        if what == "z":
            for i in range(2):
                needs = ["qa%d" % i, "qb%d" % k]
                if k >= 2:
                    needs += [p + "%d%d" % (k - 2, 2 * i + s) for p in "hr" for s in (0, 1)]
                mm("z%d%d" % (k, i), needs, bk("pz", 2 * (k % 2) + i), "ac", "as", i, "bc", "bs", k, True, True)
        elif what == "d":
            for b in bs:
                needs = ["qS%d" % b, "qq%d" % k] + (["e%d%d" % (k - 1, b)] if k else [])
                mm("d%d%d" % (k, b), needs, bk("pd", b), "sc", "ss", b, "qc", "qs", k, True, True)
        else:
            kind, r = SLICES[k][0], ranks[SLICES[k][1]]
            buf, j, need = ("u", 3, "qu3") if r == rank else ("l" + kind, r, "a%s%d" % (kind, r))
            for b in bs:
                mm("s%d%d" % (k, b), [need] + (free if k == 0 else []), bk("pz", b), "sc", "ss", b,
                   buf + "c", buf + "s", j, k == 0, k == last)

    def send(group):
        needs = ["q%s%d" % it for it in group]
        for plane in "cs":
            def view(buf, k, plane=plane):
                v = wd(buf, k)
                return v.bitcast(dt.uint8) if plane == "c" else v

            def call(view=view, plane=plane):
                tr = []
                for kind, k in group:
                    rid, pid = topo.addr(order[k], core)
                    tr.append(RemoteDMATransfer(
                        dst_ids=[DstId(rid=rid, pnc=pid)], dma_engine_mask=masks[(kind, k)], remote_sem=T.sem["a%s%d" % (kind, rank)],
                        src=view(kind + plane, k), dst=view("l" + kind + plane, rank)))
                return g.remote_dma_fused(tr, local_sem=T.sem.loc)
            op("pool", "", needs, call, sig=False)
            count["loc"] = count.get("loc", 0) + sum(len(bits(masks[it])) for it in group)

    for group in SENDS:
        send(group)

    for b in range(4):
        op("dve", "y%d" % b, ["s%d%d" % (last, b), "dcopy%d" % b], lambda b=b: g.vector.tensor_tensor(
            tb("yt", 0, b), tb("df", 0, b), bk("pz", b), AluOpType.add))
    op("sync", "st", ["y%d" % b for b in range(4)], lambda: g.sync.dma_start(T.y[:], T.yt[:]), sem="st", n=16)

    tok["loc"] = ("loc", count["loc"])
    op("pool", "", ["loc"], None, sig=False)
    op("sync", "", ["st"], None, sig=False)

    emit(T, queues, progs, tok)


def emit(T, queues, progs, tok):
    known = {q: {} for q in queues}
    clock = {sv: {sv[0]: sv[1]} for sv in tok.values() if sv[0][:2] in ("aq", "au", "lo")}
    at = {q: 0 for q in queues}
    left = sum(len(p) for p in progs.values())
    while left:
        moved = False
        for q in queues:
            while at[q] < len(progs[q]):
                label, needs, call, sig = progs[q][at[q]]
                want = {}
                for n in needs:
                    s, v = tok[n]
                    want[s] = max(v, want.get(s, 0))
                if any(sv not in clock for sv in want.items()):
                    break
                have = known[q]
                for s, v in sorted(want.items(), key=lambda x: -len(clock[x])):
                    if have.get(s, 0) < v:
                        queues[q].wait_ge(T.sem[s], v)
                        for s2, v2 in clock[(s, v)].items():
                            have[s2] = max(v2, have.get(s2, 0))
                if call is not None:
                    ins = call()
                    if sig is not None:
                        ins.then_inc(T.sem[sig[0]], sig[1])
                        c = dict(have)
                        c[sig[0]] = max(c.get(sig[0], 0), tok[label][1])
                        clock[tok[label]] = c
                at[q] += 1
                left -= 1
                moved = True
        if not moved:
            raise RuntimeError("the queues wait for one another: " + ", ".join(
                progs[q][at[q]][0] for q in queues if at[q] < len(progs[q])))
